import numpy as np
import ml_dtypes


def mxq(x, axis, fmt="e4m3"):
    dtype, down = {"e4m3": (ml_dtypes.float8_e4m3fn, 7), "e5m2": (ml_dtypes.float8_e5m2, 14)}[fmt]
    v = np.moveaxis(np.asarray(x, np.float32).astype(ml_dtypes.bfloat16).astype(np.float64), axis, -1)
    blocks = v.reshape(v.shape[:-1] + (-1, 32))
    amax = np.abs(blocks).max(-1, keepdims=True)
    byte = np.maximum(np.where(amax > 0, np.frexp(amax)[1] - 1 + 127, 0) - down, 1)
    scale = np.exp2(byte - 127.0)
    codes = (blocks / scale).astype(np.float32).astype(dtype).astype(np.float64)
    return np.moveaxis((codes * scale).reshape(v.shape), -1, axis)


WIDE = False


def mx_kscale(k):
    if not WIDE:
        return np.ones(k)
    levels = np.array([10, -10, 5, -5, 0])
    if k % 512:
        return np.exp2(np.random.permutation(np.resize(levels, k // 32))).repeat(32)
    a = np.empty((k // 512, 16))
    for p in range(k // 512):
        a[p, :8] = np.random.permutation(np.resize(levels, 8))
        for g in range(8):
            far = levels[np.abs(levels - a[p, g]) >= 10]
            a[p, g + 8] = far[np.random.randint(len(far))]
    return np.exp2(a.ravel()).repeat(32)


def f64(x):
    return np.asarray(x).astype(np.float64)


def striped8(idx):
    return np.concatenate([v.reshape(-1, 16).T for v in idx]).astype(np.uint16)


def unstriped8(offs):
    return np.stack([offs[16 * g:16 * g + 16].T.reshape(-1) for g in range(8)]).astype(np.int64)


def gelu(v):
    return 0.5 * v * (1.0 + np.tanh(np.sqrt(2.0 / np.pi) * (v + 0.044715 * v**3)))


K, M, T, S = 1024, 256, 4096, 2048


def setup_inputs():
    n = np.random.standard_normal
    s = mx_kscale(K)[:, None]
    return {
        "x": (n((K, S)) * s).astype(np.float32),
        "w": (n((K, M)) / np.sqrt(K) / s).astype(np.float32),
        "b": (0.3 * n(256)).astype(np.float32),
        "wgo": np.repeat(np.random.uniform(0.5, 2.0, (8, S)), 16, axis=0).astype(np.float32),
        "offs": striped8(np.stack([np.random.permutation(T)[:S] for _ in range(8)])),
    }


def reference(x, w, b, wgo, offs):
    x_ = mxq(f64(x), 0, "e4m3")
    w_ = mxq(f64(w), 0, "e4m3")
    y = w_.T @ x_
    place = unstriped8(offs)[np.arange(M) % 128 // 16]
    out = np.zeros((M, T))
    out[np.arange(M)[:, None], place] = f64(wgo)[np.arange(M) % 128] * (gelu(y + f64(b)[:, None]))
    return out

@@ -1,0 +1,172 @@
+from contextlib import ExitStack
+
+import concourse.mybir as mybir
+
+K, M, T, S = 1024, 256, 4096, 2048
+FLOPS = 2 * K * M * S
+
+F32 = mybir.dt.float32
+BF16 = mybir.dt.bfloat16
+U32 = mybir.dt.uint32
+U16 = mybir.dt.uint16
+U8 = mybir.dt.uint8
+FP8X4 = mybir.dt.float8_e4m3fn_x4
+GELU = mybir.ActivationFunctionType.Gelu_apprx_tanh
+MULT = mybir.AluOpType.mult
+
+P = 128
+PACK = 4
+K_PASS = P * PACK
+PASSES = K // K_PASS
+M_TILES = M // P
+PIECE = 1024
+PIECES = S // PIECE
+
+
+def interleave(copy, grouped, raw, c0, c1):
+    copy(
+        out=grouped[:, c0:c1, :].rearrange("p (c i) j -> p c j i", i=4),
+        in_=raw[:, :, c0:c1].rearrange("p j (c i) -> p c j i", i=4),
+    )
+
+
+def tile_list_hscat_gelu_kernel(tc, x, w, b, wgo, offs, out):
+    nc = tc.nc
+    with ExitStack() as ctx:
+        keep = ctx.enter_context(tc.tile_pool(name="keep", bufs=1))
+        psum = ctx.enter_context(tc.psum_pool(name="psum", bufs=8))
+
+        offsets = keep.tile([P, S // 16], U16, name="offsets")
+
+        warm = keep.tile([P, 1], F32, name="warm")
+        nc.gpsimd.memset(warm[:], 0.0)
+        warmed = keep.tile([P, 1], F32, name="warmed")
+        nc.scalar.activation(out=warmed[:], in_=warm[:], func=GELU)
+
+        bias = keep.tile([P, M_TILES], F32, name="bias")
+        with nc.allow_non_contiguous_dma(reason="one bias value to a partition"):
+            nc.scalar.dma_start(out=bias[:], in_=b.rearrange("(m p) -> p m", p=P))
+
+        blocks = [(0, 512), (512, 256), (768, 256), (1024, 512), (1536, 256), (1792, 256)]
+        loads = [
+            (0, 0, 512), (1, 0, 512), (0, 512, 512), (1, 512, 256), (1, 768, 256),
+            (0, 1024, 512), (1, 1024, 512), (0, 1536, 512), (1, 1536, 512),
+        ]
+
+        w_raw = keep.tile([P, PASSES, PACK, M], F32, name="w_raw")
+        nc.sync.dma_start(
+            out=w_raw[:].rearrange("p a j n -> p a (j n)"),
+            in_=w.rearrange("(a p j) n -> p a (j n)", a=PASSES, j=PACK),
+        )
+        raws = []
+        weights_out = []
+        for (a, c0, width) in loads:
+            raw = keep.tile([P, PACK, width], F32, name=f"raw_{a}_{c0}")
+            nc.sync.dma_start(
+                out=raw[:],
+                in_=x[a * K_PASS : (a + 1) * K_PASS, c0 : c0 + width].rearrange("(p j) c -> p j c", j=PACK),
+            )
+            raws.append(raw)
+            if (a, c0) == (1, 768):
+                nc.sync.dma_start(out=offsets[:], in_=offs)
+                wg = keep.tile([P, PIECE], F32, name="wgo_0")
+                nc.sync.dma_start(out=wg[:], in_=wgo[:, 0:PIECE])
+                weights_out.append(wg)
+        wg = keep.tile([P, PIECE], F32, name="wgo_1")
+        nc.sync.dma_start(out=wg[:], in_=wgo[:, PIECE : 2 * PIECE])
+        weights_out.append(wg)
+
+        placed = []
+        for m in range(M_TILES):
+            window = keep.tile([P, T], F32, name=f"placed_{m}")
+            nc.vector.memset(window[:], 0.0)
+            placed.append(window)
+
+        w_grouped = keep.tile([P, PASSES, M, PACK], BF16, name="w_grouped", align_bytes=64)
+        for a in range(PASSES):
+            interleave(nc.scalar.copy, w_grouped[:, a, :, :], w_raw[:, a, :, :], 0, M)
+        w_codes = keep.tile([P, PASSES * M], U32, name="w_codes", align_bytes=64)
+        w_scales = keep.tile([P, PASSES * M], U8, name="w_scales", align_bytes=64)
+        nc.vector.quantize_mx(
+            out=w_codes[:].bitcast(FP8X4), scales=w_scales[:], in_=w_grouped[:].rearrange("p a n j -> p (a n j)")
+        )
+
+        x_codes = [keep.tile([P, S], U32, name=f"x_codes_{a}", align_bytes=64) for a in range(PASSES)]
+        x_scales = [keep.tile([P, S], U8, name=f"x_scales_{a}", align_bytes=64) for a in range(PASSES)]
+        groupeds = [
+            keep.tile([P, width, PACK], BF16, name=f"grouped_{a}_{c0}", align_bytes=64) for (a, c0, width) in loads
+        ]
+
+        def copy_in(i, vector_columns):
+            width = loads[i][2]
+            if vector_columns > 0:
+                interleave(nc.vector.tensor_copy, groupeds[i], raws[i], 0, vector_columns)
+            if vector_columns < width:
+                interleave(nc.scalar.copy, groupeds[i], raws[i], vector_columns, width)
+
+        def quantize(i, q0, q1):
+            a, c0, width = loads[i]
+            nc.vector.quantize_mx(
+                out=x_codes[a][:, c0 + q0 : c0 + q1].bitcast(FP8X4),
+                scales=x_scales[a][:, c0 + q0 : c0 + q1],
+                in_=groupeds[i][:, q0:q1, :].rearrange("p c j -> p (c j)"),
+            )
+
+        results = [keep.tile([P, S], F32, name=f"results_{m}") for m in range(M_TILES)]
+
+        def multiply(m, c0, width):
+            acc = psum.tile([P, 512], F32, name="acc")
+            for a in range(PASSES):
+                w_cols = slice(a * M + m * P, a * M + (m + 1) * P)
+                nc.tensor.matmul_mx(
+                    out=acc[:, 0:width],
+                    lhsT=w_codes[:, w_cols].bitcast(FP8X4),
+                    lhsT_scale=w_scales[:, w_cols],
+                    rhs=x_codes[a][:, c0 : c0 + width].bitcast(FP8X4),
+                    rhs_scale=x_scales[a][:, c0 : c0 + width],
+                    start=(a == 0),
+                    stop=(a == PASSES - 1),
+                )
+            nc.scalar.activation(
+                out=results[m][:, c0 : c0 + width], in_=acc[:, 0:width], func=GELU, bias=bias[:, m : m + 1]
+            )
+
+        def place(m, h):
+            nc.vector.tensor_tensor(
+                placed[m][:].indirect(offsets[:, h * (PIECE // 16) : (h + 1) * (PIECE // 16)]),
+                results[m][:, h * PIECE : (h + 1) * PIECE],
+                weights_out[h][:],
+                MULT,
+            )
+
+        for i, vc in ((0, 320), (1, 320), (2, 320), (3, 160), (4, 128)):
+            copy_in(i, vc)
+            quantize(i, 0, loads[i][2])
+            if i == 1:
+                multiply(0, 0, 512)
+            if i == 3:
+                multiply(0, 512, 256)
+        multiply(0, 768, 256)
+        place(0, 0)
+        for c0, width in blocks[0:3]:
+            multiply(1, c0, width)
+
+        copy_in(5, 0)
+        quantize(5, 0, 512)
+        copy_in(6, 0)
+        quantize(6, 0, 512)
+        place(1, 0)
+        multiply(0, 1024, 512)
+        copy_in(7, 0)
+        quantize(7, 0, 512)
+        copy_in(8, 0)
+        quantize(8, 0, 256)
+        multiply(0, 1536, 256)
+        quantize(8, 256, 512)
+        multiply(0, 1792, 256)
+        place(0, 1)
+        nc.sync.dma_start(out=out[0:P, :], in_=placed[0][:])
+        for c0, width in blocks[3:6]:
+            multiply(1, c0, width)
+        place(1, 1)
+        nc.sync.dma_start(out=out[P : 2 * P, :], in_=placed[1][:])

@@ -21,6 +21,7 @@ PASSES = K // K_PASS
 M_TILES = M // P
 PIECE = 1024
 PIECES = S // PIECE
+SHARED = {(1, 768): "last_0", (1, 1536): "last_1"}
 
 
 def interleave(copy, grouped, raw, c0, c1):
@@ -34,7 +35,7 @@ def tile_list_hscat_gelu_kernel(tc, x, w, b, wgo, offs, out):
     nc = tc.nc
     with ExitStack() as ctx:
         keep = ctx.enter_context(tc.tile_pool(name="keep", bufs=1))
-        psum = ctx.enter_context(tc.psum_pool(name="psum", bufs=8))
+        psum = ctx.enter_context(tc.psum_pool(name="psum", bufs=1))
 
         offsets = keep.tile([P, S // 16], U16, name="offsets")
 
@@ -47,7 +48,6 @@ def tile_list_hscat_gelu_kernel(tc, x, w, b, wgo, offs, out):
         with nc.allow_non_contiguous_dma(reason="one bias value to a partition"):
             nc.scalar.dma_start(out=bias[:], in_=b.rearrange("(m p) -> p m", p=P))
 
-        blocks = [(0, 512), (512, 256), (768, 256), (1024, 512), (1536, 256), (1792, 256)]
         loads = [
             (0, 0, 512), (1, 0, 512), (0, 512, 512), (1, 512, 256), (1, 768, 256),
             (0, 1024, 512), (1, 1024, 512), (0, 1536, 512), (1, 1536, 512),
@@ -61,7 +61,7 @@ def tile_list_hscat_gelu_kernel(tc, x, w, b, wgo, offs, out):
         raws = []
         weights_out = []
         for (a, c0, width) in loads:
-            raw = keep.tile([P, PACK, width], F32, name=f"raw_{a}_{c0}")
+            raw = keep.tile([P, PACK, width], F32, name=f"raw_{a}_{c0}", tag=SHARED.get((a, c0), f"raw_{a}_{c0}"))
             nc.sync.dma_start(
                 out=raw[:],
                 in_=x[a * K_PASS : (a + 1) * K_PASS, c0 : c0 + width].rearrange("(p j) c -> p j c", j=PACK),
@@ -79,7 +79,7 @@ def tile_list_hscat_gelu_kernel(tc, x, w, b, wgo, offs, out):
         placed = []
         for m in range(M_TILES):
             window = keep.tile([P, T], F32, name=f"placed_{m}")
-            nc.vector.memset(window[:], 0.0)
+            (nc.vector if m == 0 else nc.gpsimd).memset(window[:], 0.0)
             placed.append(window)
 
         w_grouped = keep.tile([P, PASSES, M, PACK], BF16, name="w_grouped", align_bytes=64)
@@ -112,14 +112,27 @@ def tile_list_hscat_gelu_kernel(tc, x, w, b, wgo, offs, out):
                 in_=groupeds[i][:, q0:q1, :].rearrange("p c j -> p (c j)"),
             )
 
-        results = [keep.tile([P, S], F32, name=f"results_{m}") for m in range(M_TILES)]
+        results = {}
+        sums = {}
 
-        def multiply(m, c0, width):
-            acc = psum.tile([P, 512], F32, name="acc")
+        def multiply(m, h, c0, width):
+            if (m, h) not in results:
+                results[(m, h)] = keep.tile([P, PIECE], F32, name=f"results_{m}_{h}", tag=f"last_{h}" if m == 0 else f"results_{m}_{h}")
+            local = c0 - h * PIECE
+            if m == 0 and local < 768:
+                acc_tile = psum.tile([P, 512], F32, name=f"acc_{local}")
+                acc = acc_tile[:, 0:width]
+            elif m == 0:
+                acc_tile = psum.tile([P, 1024], F32, name=f"acc_last_{h}", tag="late")
+                acc = acc_tile[:, 0:width]
+            else:
+                if h not in sums:
+                    sums[h] = psum.tile([P, 1024], F32, name=f"acc_1_{h}", tag="late")
+                acc = sums[h][:, local : local + width]
             for a in range(PASSES):
                 w_cols = slice(a * M + m * P, a * M + (m + 1) * P)
                 nc.tensor.matmul_mx(
-                    out=acc[:, 0:width],
+                    out=acc,
                     lhsT=w_codes[:, w_cols].bitcast(FP8X4),
                     lhsT_scale=w_scales[:, w_cols],
                     rhs=x_codes[a][:, c0 : c0 + width].bitcast(FP8X4),
@@ -128,13 +141,13 @@ def tile_list_hscat_gelu_kernel(tc, x, w, b, wgo, offs, out):
                     stop=(a == PASSES - 1),
                 )
             nc.scalar.activation(
-                out=results[m][:, c0 : c0 + width], in_=acc[:, 0:width], func=GELU, bias=bias[:, m : m + 1]
+                out=results[(m, h)][:, local : local + width], in_=acc, func=GELU, bias=bias[:, m : m + 1]
             )
 
         def place(m, h):
             nc.vector.tensor_tensor(
                 placed[m][:].indirect(offsets[:, h * (PIECE // 16) : (h + 1) * (PIECE // 16)]),
-                results[m][:, h * PIECE : (h + 1) * PIECE],
+                results[(m, h)][:],
                 weights_out[h][:],
                 MULT,
             )
@@ -142,31 +155,25 @@ def tile_list_hscat_gelu_kernel(tc, x, w, b, wgo, offs, out):
         for i, vc in ((0, 320), (1, 320), (2, 320), (3, 160), (4, 128)):
             copy_in(i, vc)
             quantize(i, 0, loads[i][2])
-            if i == 1:
-                multiply(0, 0, 512)
-            if i == 3:
-                multiply(0, 512, 256)
-        multiply(0, 768, 256)
+        for c0, width in ((0, 512), (512, 256), (768, 256)):
+            multiply(0, 0, c0, width)
         place(0, 0)
-        for c0, width in blocks[0:3]:
-            multiply(1, c0, width)
+        for c0 in (0, 512):
+            multiply(1, 0, c0, 512)
 
-        copy_in(5, 0)
+        for i in (5, 6, 7, 8):
+            copy_in(i, 0)
         quantize(5, 0, 512)
-        copy_in(6, 0)
         quantize(6, 0, 512)
         place(1, 0)
-        multiply(0, 1024, 512)
-        copy_in(7, 0)
         quantize(7, 0, 512)
-        copy_in(8, 0)
         quantize(8, 0, 256)
-        multiply(0, 1536, 256)
         quantize(8, 256, 512)
-        multiply(0, 1792, 256)
+        for c0, width in ((1024, 512), (1536, 256), (1792, 256)):
+            multiply(0, 1, c0, width)
         place(0, 1)
         nc.sync.dma_start(out=out[0:P, :], in_=placed[0][:])
-        for c0, width in blocks[3:6]:
-            multiply(1, c0, width)
+        for c0 in (1024, 1536):
+            multiply(1, 1, c0, 512)
         place(1, 1)
         nc.sync.dma_start(out=out[P : 2 * P, :], in_=placed[1][:])

@@ -21,7 +21,7 @@ PASSES = K // K_PASS
 M_TILES = M // P
 PIECE = 1024
 PIECES = S // PIECE
-SHARED = {(1, 768): "last_0", (1, 1536): "last_1"}
+SHARED = {(1, 896): "last_0", (1, 1536): "last_1"}
 
 
 def interleave(copy, grouped, raw, c0, c1):
@@ -49,7 +49,7 @@ def tile_list_hscat_gelu_kernel(tc, x, w, b, wgo, offs, out):
             nc.scalar.dma_start(out=bias[:], in_=b.rearrange("(m p) -> p m", p=P))
 
         loads = [
-            (0, 0, 512), (1, 0, 512), (0, 512, 512), (1, 512, 256), (1, 768, 256),
+            (0, 0, 1024), (1, 0, 512), (1, 512, 384), (1, 896, 128),
             (0, 1024, 512), (1, 1024, 512), (0, 1536, 512), (1, 1536, 512),
         ]
 
@@ -67,7 +67,7 @@ def tile_list_hscat_gelu_kernel(tc, x, w, b, wgo, offs, out):
                 in_=x[a * K_PASS : (a + 1) * K_PASS, c0 : c0 + width].rearrange("(p j) c -> p j c", j=PACK),
             )
             raws.append(raw)
-            if (a, c0) == (1, 768):
+            if (a, c0) == (1, 896):
                 nc.sync.dma_start(out=offsets[:], in_=offs)
                 wg = keep.tile([P, PIECE], F32, name="wgo_0")
                 nc.sync.dma_start(out=wg[:], in_=wgo[:, 0:PIECE])
@@ -97,12 +97,11 @@ def tile_list_hscat_gelu_kernel(tc, x, w, b, wgo, offs, out):
             keep.tile([P, width, PACK], BF16, name=f"grouped_{a}_{c0}", align_bytes=64) for (a, c0, width) in loads
         ]
 
-        def copy_in(i, vector_columns):
-            width = loads[i][2]
+        def copy_in(i, c0, c1, vector_columns):
             if vector_columns > 0:
-                interleave(nc.vector.tensor_copy, groupeds[i], raws[i], 0, vector_columns)
-            if vector_columns < width:
-                interleave(nc.scalar.copy, groupeds[i], raws[i], vector_columns, width)
+                interleave(nc.vector.tensor_copy, groupeds[i], raws[i], c0, c0 + vector_columns)
+            if c0 + vector_columns < c1:
+                interleave(nc.scalar.copy, groupeds[i], raws[i], c0 + vector_columns, c1)
 
         def quantize(i, q0, q1):
             a, c0, width = loads[i]
@@ -119,7 +118,7 @@ def tile_list_hscat_gelu_kernel(tc, x, w, b, wgo, offs, out):
             if (m, h) not in results:
                 results[(m, h)] = keep.tile([P, PIECE], F32, name=f"results_{m}_{h}", tag=f"last_{h}" if m == 0 else f"results_{m}_{h}")
             local = c0 - h * PIECE
-            if m == 0 and local < 768:
+            if m == 0 and local < 896:
                 acc_tile = psum.tile([P, 512], F32, name=f"acc_{local}")
                 acc = acc_tile[:, 0:width]
             elif m == 0:
@@ -152,24 +151,33 @@ def tile_list_hscat_gelu_kernel(tc, x, w, b, wgo, offs, out):
                 MULT,
             )
 
-        for i, vc in ((0, 320), (1, 320), (2, 320), (3, 160), (4, 128)):
-            copy_in(i, vc)
-            quantize(i, 0, loads[i][2])
-        for c0, width in ((0, 512), (512, 256), (768, 256)):
+        copy_in(0, 0, 512, 320)
+        quantize(0, 0, 512)
+        copy_in(0, 512, 1024, 320)
+        quantize(0, 512, 1024)
+        copy_in(1, 0, 512, 320)
+        quantize(1, 0, 512)
+        copy_in(2, 0, 384, 224)
+        quantize(2, 0, 256)
+        quantize(2, 256, 384)
+        copy_in(3, 0, 128, 64)
+        quantize(3, 0, 128)
+        for c0, width in ((0, 512), (512, 256), (768, 128), (896, 128)):
             multiply(0, 0, c0, width)
         place(0, 0)
         for c0 in (0, 512):
             multiply(1, 0, c0, 512)
 
-        for i in (5, 6, 7, 8):
-            copy_in(i, 0)
+        for i in (4, 5, 6, 7):
+            copy_in(i, 0, 512, 0)
+        quantize(4, 0, 512)
+        place(1, 0)
         quantize(5, 0, 512)
         quantize(6, 0, 512)
-        place(1, 0)
-        quantize(7, 0, 512)
-        quantize(8, 0, 256)
-        quantize(8, 256, 512)
-        for c0, width in ((1024, 512), (1536, 256), (1792, 256)):
+        quantize(7, 0, 256)
+        quantize(7, 256, 384)
+        quantize(7, 384, 512)
+        for c0, width in ((1024, 512), (1536, 256), (1792, 128), (1920, 128)):
             multiply(0, 1, c0, width)
         place(0, 1)
         nc.sync.dma_start(out=out[0:P, :], in_=placed[0][:])

@@ -1,6 +1,7 @@
 from contextlib import ExitStack
 
 import concourse.mybir as mybir
+from concourse.masks import make_identity
 
 K, M, T, S = 1024, 256, 4096, 2048
 FLOPS = 2 * K * M * S
@@ -44,9 +45,15 @@ def tile_list_hscat_gelu_kernel(tc, x, w, b, wgo, offs, out):
         warmed = keep.tile([P, 1], F32, name="warmed")
         nc.scalar.activation(out=warmed[:], in_=warm[:], func=GELU)
 
+        identity = keep.tile([P, P], F32, name="identity")
+        make_identity(nc, identity[:])
+        b_rows = keep.tile([P, P], F32, name="b_rows")
+        nc.gpsimd.memset(b_rows[:], 0.0)
+        nc.scalar.dma_start(out=b_rows[0:M_TILES, :], in_=b.rearrange("(m p) -> m p", p=P))
+        b_turned = psum.tile([P, P], F32, name="b_turned")
+        nc.tensor.transpose(b_turned[:], b_rows[:], identity[:])
         bias = keep.tile([P, M_TILES], F32, name="bias")
-        with nc.allow_non_contiguous_dma(reason="one bias value to a partition"):
-            nc.scalar.dma_start(out=bias[:], in_=b.rearrange("(m p) -> p m", p=P))
+        nc.scalar.copy(out=bias[:], in_=b_turned[:, 0:M_TILES])
 
         loads = [
             (0, 0, 1024), (1, 0, 512), (1, 512, 384), (1, 896, 128),

@@ -19,10 +19,20 @@ P = 128
 PACK = 4
 K_PASS = P * PACK
 PASSES = K // K_PASS
-M_TILES = M // P
-PIECE = 1024
-PIECES = S // PIECE
-SHARED = {(1, 896): "last_0", (1, 1536): "last_1"}
+ROW_TILES = M // P
+HALF = S // 2
+HALVES = S // HALF
+LIST_COLUMNS = HALF // 16
+BANK = 512
+
+LOADS = [
+    [(0, 0, 1024), (1, 0, 512), (1, 512, 384), (1, 896, 128)],
+    [(0, 1024, 512), (1, 1024, 512), (0, 1536, 512), (1, 1536, 512)],
+]
+BLOCKS = [
+    [(0, 512), (512, 256), (768, 128), (896, 128)],
+    [(0, 512), (512, 256), (768, 128), (896, 128)],
+]
 
 
 def interleave(copy, grouped, raw, c0, c1):
@@ -40,54 +50,53 @@ def tile_list_hscat_gelu_kernel(tc, x, w, b, wgo, offs, out):
 
         offsets = keep.tile([P, S // 16], U16, name="offsets")
 
-        warm = keep.tile([P, 1], F32, name="warm")
-        nc.gpsimd.memset(warm[:], 0.0)
-        warmed = keep.tile([P, 1], F32, name="warmed")
-        nc.scalar.activation(out=warmed[:], in_=warm[:], func=GELU)
+        zero = keep.tile([P, 1], F32, name="zero")
+        nc.gpsimd.memset(zero[:], 0.0)
+        table_loaded = keep.tile([P, 1], F32, name="table_loaded")
+        nc.scalar.activation(out=table_loaded[:], in_=zero[:], func=GELU)
 
         identity = keep.tile([P, P], F32, name="identity")
         make_identity(nc, identity[:])
         b_rows = keep.tile([P, P], F32, name="b_rows")
         nc.gpsimd.memset(b_rows[:], 0.0)
-        nc.scalar.dma_start(out=b_rows[0:M_TILES, :], in_=b.rearrange("(m p) -> m p", p=P))
+        nc.scalar.dma_start(out=b_rows[0:ROW_TILES, :], in_=b.rearrange("(m p) -> m p", p=P))
         b_turned = psum.tile([P, P], F32, name="b_turned")
         nc.tensor.transpose(b_turned[:], b_rows[:], identity[:])
-        bias = keep.tile([P, M_TILES], F32, name="bias")
-        nc.scalar.copy(out=bias[:], in_=b_turned[:, 0:M_TILES])
-
-        loads = [
-            (0, 0, 1024), (1, 0, 512), (1, 512, 384), (1, 896, 128),
-            (0, 1024, 512), (1, 1024, 512), (0, 1536, 512), (1, 1536, 512),
-        ]
 
         w_raw = keep.tile([P, PASSES, PACK, M], F32, name="w_raw")
         nc.sync.dma_start(
-            out=w_raw[:].rearrange("p a j n -> p a (j n)"),
-            in_=w.rearrange("(a p j) n -> p a (j n)", a=PASSES, j=PACK),
+            out=w_raw[:].rearrange("p a i n -> p a (i n)"),
+            in_=w.rearrange("(a p i) n -> p a (i n)", a=PASSES, i=PACK),
         )
-        raws = []
-        weights_out = []
-        for (a, c0, width) in loads:
-            raw = keep.tile([P, PACK, width], F32, name=f"raw_{a}_{c0}", tag=SHARED.get((a, c0), f"raw_{a}_{c0}"))
-            nc.sync.dma_start(
-                out=raw[:],
-                in_=x[a * K_PASS : (a + 1) * K_PASS, c0 : c0 + width].rearrange("(p j) c -> p j c", j=PACK),
-            )
-            raws.append(raw)
-            if (a, c0) == (1, 896):
+        raws = {}
+        factors = []
+        for h in range(HALVES):
+            for load in LOADS[h]:
+                a, c0, width = load
+                if load == LOADS[h][-1]:
+                    tag = f"last_{h}"
+                elif load == LOADS[0][-2]:
+                    tag = "last_but_one"
+                else:
+                    tag = f"raw_{a}_{c0}"
+                raw = keep.tile([P, PACK, width], F32, name=f"raw_{a}_{c0}", tag=tag)
+                nc.sync.dma_start(
+                    out=raw[:],
+                    in_=x[a * K_PASS : (a + 1) * K_PASS, c0 : c0 + width].rearrange("(p i) c -> p i c", i=PACK),
+                )
+                raws[load] = raw
+            if h == 0:
                 nc.sync.dma_start(out=offsets[:], in_=offs)
-                wg = keep.tile([P, PIECE], F32, name="wgo_0")
-                nc.sync.dma_start(out=wg[:], in_=wgo[:, 0:PIECE])
-                weights_out.append(wg)
-        wg = keep.tile([P, PIECE], F32, name="wgo_1")
-        nc.sync.dma_start(out=wg[:], in_=wgo[:, PIECE : 2 * PIECE])
-        weights_out.append(wg)
+            factor = keep.tile([P, HALF], F32, name=f"factor_{h}")
+            if h == 0:
+                nc.sync.dma_start(out=factor[:], in_=wgo[:, 0:HALF])
+            else:
+                nc.sync.dma_start(out=factor[:], in_=wgo[:, HALF:S])
+            factors.append(factor)
 
-        placed = []
-        for m in range(M_TILES):
-            window = keep.tile([P, T], F32, name=f"placed_{m}")
-            (nc.vector if m == 0 else nc.gpsimd).memset(window[:], 0.0)
-            placed.append(window)
+        placed = [keep.tile([P, T], F32, name=f"placed_{m}") for m in range(ROW_TILES)]
+        nc.vector.memset(placed[0][:], 0.0)
+        nc.gpsimd.memset(placed[1][:], 0.0)
 
         w_grouped = keep.tile([P, PASSES, M, PACK], BF16, name="w_grouped", align_bytes=64)
         for a in range(PASSES):
@@ -95,100 +104,102 @@ def tile_list_hscat_gelu_kernel(tc, x, w, b, wgo, offs, out):
         w_codes = keep.tile([P, PASSES * M], U32, name="w_codes", align_bytes=64)
         w_scales = keep.tile([P, PASSES * M], U8, name="w_scales", align_bytes=64)
         nc.vector.quantize_mx(
-            out=w_codes[:].bitcast(FP8X4), scales=w_scales[:], in_=w_grouped[:].rearrange("p a n j -> p (a n j)")
+            out=w_codes[:].bitcast(FP8X4),
+            scales=w_scales[:],
+            in_=w_grouped[:].rearrange("p a n i -> p (a n i)"),
         )
 
         x_codes = [keep.tile([P, S], U32, name=f"x_codes_{a}", align_bytes=64) for a in range(PASSES)]
         x_scales = [keep.tile([P, S], U8, name=f"x_scales_{a}", align_bytes=64) for a in range(PASSES)]
-        groupeds = [
-            keep.tile([P, width, PACK], BF16, name=f"grouped_{a}_{c0}", align_bytes=64) for (a, c0, width) in loads
-        ]
+        grouped = {}
+        for h in range(HALVES):
+            for load in LOADS[h]:
+                a, c0, width = load
+                grouped[load] = keep.tile([P, width, PACK], BF16, name=f"grouped_{a}_{c0}", align_bytes=64)
 
-        def copy_in(i, c0, c1, vector_columns):
+        def copy_in(load, c0, c1, vector_columns):
+            split = c0 + vector_columns
             if vector_columns > 0:
-                interleave(nc.vector.tensor_copy, groupeds[i], raws[i], c0, c0 + vector_columns)
-            if c0 + vector_columns < c1:
-                interleave(nc.scalar.copy, groupeds[i], raws[i], c0 + vector_columns, c1)
+                interleave(nc.vector.tensor_copy, grouped[load], raws[load], c0, split)
+            interleave(nc.scalar.copy, grouped[load], raws[load], split, c1)
 
-        def quantize(i, q0, q1):
-            a, c0, width = loads[i]
+        def quantize(load, c0, c1):
+            a, first, width = load
             nc.vector.quantize_mx(
-                out=x_codes[a][:, c0 + q0 : c0 + q1].bitcast(FP8X4),
-                scales=x_scales[a][:, c0 + q0 : c0 + q1],
-                in_=groupeds[i][:, q0:q1, :].rearrange("p c j -> p (c j)"),
+                out=x_codes[a][:, first + c0 : first + c1].bitcast(FP8X4),
+                scales=x_scales[a][:, first + c0 : first + c1],
+                in_=grouped[load][:, c0:c1, :].rearrange("p c i -> p (c i)"),
             )
 
-        results = {}
-        sums = {}
+        bias = keep.tile([P, ROW_TILES], F32, name="bias", tag="last_but_one")
 
-        def multiply(m, h, c0, width):
-            if (m, h) not in results:
-                results[(m, h)] = keep.tile([P, PIECE], F32, name=f"results_{m}_{h}", tag=f"last_{h}" if m == 0 else f"results_{m}_{h}")
-            local = c0 - h * PIECE
-            if m == 0 and local < 896:
-                acc_tile = psum.tile([P, 512], F32, name=f"acc_{local}")
-                acc = acc_tile[:, 0:width]
-            elif m == 0:
-                acc_tile = psum.tile([P, 1024], F32, name=f"acc_last_{h}", tag="late")
-                acc = acc_tile[:, 0:width]
-            else:
-                if h not in sums:
-                    sums[h] = psum.tile([P, 1024], F32, name=f"acc_1_{h}", tag="late")
-                acc = sums[h][:, local : local + width]
+        def multiply(m, sums, results, h, c0, width):
             for a in range(PASSES):
                 w_cols = slice(a * M + m * P, a * M + (m + 1) * P)
+                x_cols = slice(h * HALF + c0, h * HALF + c0 + width)
                 nc.tensor.matmul_mx(
-                    out=acc,
+                    out=sums,
                     lhsT=w_codes[:, w_cols].bitcast(FP8X4),
                     lhsT_scale=w_scales[:, w_cols],
-                    rhs=x_codes[a][:, c0 : c0 + width].bitcast(FP8X4),
-                    rhs_scale=x_scales[a][:, c0 : c0 + width],
+                    rhs=x_codes[a][:, x_cols].bitcast(FP8X4),
+                    rhs_scale=x_scales[a][:, x_cols],
                     start=(a == 0),
                     stop=(a == PASSES - 1),
                 )
-            nc.scalar.activation(
-                out=results[(m, h)][:, local : local + width], in_=acc, func=GELU, bias=bias[:, m : m + 1]
-            )
+            nc.scalar.activation(out=results[:, c0 : c0 + width], in_=sums, func=GELU, bias=bias[:, m : m + 1])
 
-        def place(m, h):
+        def place(m, results, h):
             nc.vector.tensor_tensor(
-                placed[m][:].indirect(offsets[:, h * (PIECE // 16) : (h + 1) * (PIECE // 16)]),
-                results[(m, h)][:],
-                weights_out[h][:],
+                placed[m][:].indirect(offsets[:, h * LIST_COLUMNS : (h + 1) * LIST_COLUMNS]),
+                results[:],
+                factors[h][:],
                 MULT,
             )
 
-        copy_in(0, 0, 512, 320)
-        quantize(0, 0, 512)
-        copy_in(0, 512, 1024, 320)
-        quantize(0, 512, 1024)
-        copy_in(1, 0, 512, 320)
-        quantize(1, 0, 512)
-        copy_in(2, 0, 384, 224)
-        quantize(2, 0, 256)
-        quantize(2, 256, 384)
-        copy_in(3, 0, 128, 64)
-        quantize(3, 0, 128)
-        for c0, width in ((0, 512), (512, 256), (768, 128), (896, 128)):
-            multiply(0, 0, c0, width)
-        place(0, 0)
-        for c0 in (0, 512):
-            multiply(1, 0, c0, 512)
+        def first_row_tile(h):
+            results = keep.tile([P, HALF], F32, name=f"results_0_{h}", tag=f"last_{h}")
+            for block in BLOCKS[h]:
+                c0, width = block
+                if block == BLOCKS[h][-1]:
+                    sums = psum.tile([P, HALF], F32, name=f"sums_0_{h}_last", tag="late")
+                else:
+                    sums = psum.tile([P, BANK], F32, name=f"sums_0_{h}_{c0}", tag=f"sums_{c0}")
+                multiply(0, sums[:, 0:width], results, h, c0, width)
+            return results
 
-        for i in (4, 5, 6, 7):
-            copy_in(i, 0, 512, 0)
-        quantize(4, 0, 512)
-        place(1, 0)
-        quantize(5, 0, 512)
-        quantize(6, 0, 512)
-        quantize(7, 0, 256)
-        quantize(7, 256, 384)
-        quantize(7, 384, 512)
-        for c0, width in ((1024, 512), (1536, 256), (1792, 128), (1920, 128)):
-            multiply(0, 1, c0, width)
-        place(0, 1)
+        def second_row_tile(h):
+            results = keep.tile([P, HALF], F32, name=f"results_1_{h}")
+            sums = psum.tile([P, HALF], F32, name=f"sums_1_{h}", tag="late")
+            for c0 in range(0, HALF, BANK):
+                multiply(1, sums[:, c0 : c0 + BANK], results, h, c0, BANK)
+            return results
+
+        whole, wide, narrow, last = LOADS[0]
+        copy_in(whole, 0, 512, 320)
+        quantize(whole, 0, 512)
+        copy_in(whole, 512, 1024, 320)
+        quantize(whole, 512, 1024)
+        copy_in(wide, 0, 512, 320)
+        quantize(wide, 0, 512)
+        copy_in(narrow, 0, 384, 224)
+        quantize(narrow, 0, 256)
+        quantize(narrow, 256, 384)
+        nc.scalar.copy(out=bias[:], in_=b_turned[:, 0:ROW_TILES])
+        copy_in(last, 0, 128, 64)
+        quantize(last, 0, 128)
+        place(0, first_row_tile(0), 0)
+        results = second_row_tile(0)
+
+        for load in LOADS[1]:
+            copy_in(load, 0, 512, 0)
+        quantize(LOADS[1][0], 0, 512)
+        place(1, results, 0)
+        quantize(LOADS[1][1], 0, 512)
+        quantize(LOADS[1][2], 0, 512)
+        quantize(LOADS[1][3], 0, 256)
+        quantize(LOADS[1][3], 256, 384)
+        quantize(LOADS[1][3], 384, 512)
+        place(0, first_row_tile(1), 1)
         nc.sync.dma_start(out=out[0:P, :], in_=placed[0][:])
-        for c0 in (1024, 1536):
-            multiply(1, 1, c0, 512)
-        place(1, 1)
-        nc.sync.dma_start(out=out[P : 2 * P, :], in_=placed[1][:])
+        place(1, second_row_tile(1), 1)
+        nc.sync.dma_start(out=out[P:M, :], in_=placed[1][:])

from contextlib import ExitStack

import concourse.mybir as mybir
from concourse.masks import make_identity

K, M, T, S = 1024, 256, 4096, 2048
FLOPS = 2 * K * M * S

F32 = mybir.dt.float32
BF16 = mybir.dt.bfloat16
U32 = mybir.dt.uint32
U16 = mybir.dt.uint16
U8 = mybir.dt.uint8
FP8X4 = mybir.dt.float8_e4m3fn_x4
GELU = mybir.ActivationFunctionType.Gelu_apprx_tanh
MULT = mybir.AluOpType.mult

P = 128
PACK = 4
K_PASS = P * PACK
PASSES = K // K_PASS
ROW_TILES = M // P
HALF = S // 2
HALVES = S // HALF
LIST_COLUMNS = HALF // 16
BANK = 512

LOADS = [
    [(0, 0, 1024), (1, 0, 512), (1, 512, 384), (1, 896, 128)],
    [(0, 1024, 512), (1, 1024, 512), (0, 1536, 512), (1, 1536, 512)],
]
BLOCKS = [
    [(0, 512), (512, 256), (768, 128), (896, 128)],
    [(0, 512), (512, 256), (768, 128), (896, 128)],
]


def interleave(copy, grouped, raw, c0, c1):
    copy(
        out=grouped[:, c0:c1, :].rearrange("p (c i) j -> p c j i", i=4),
        in_=raw[:, :, c0:c1].rearrange("p j (c i) -> p c j i", i=4),
    )


def tile_list_hscat_gelu_kernel(tc, x, w, b, wgo, offs, out):
    nc = tc.nc
    with ExitStack() as ctx:
        keep = ctx.enter_context(tc.tile_pool(name="keep", bufs=1))
        psum = ctx.enter_context(tc.psum_pool(name="psum", bufs=1))

        offsets = keep.tile([P, S // 16], U16, name="offsets")

        zero = keep.tile([P, 1], F32, name="zero")
        nc.gpsimd.memset(zero[:], 0.0)
        table_loaded = keep.tile([P, 1], F32, name="table_loaded")
        nc.scalar.activation(out=table_loaded[:], in_=zero[:], func=GELU)

        identity = keep.tile([P, P], F32, name="identity")
        make_identity(nc, identity[:])
        b_rows = keep.tile([P, P], F32, name="b_rows")
        nc.gpsimd.memset(b_rows[:], 0.0)
        nc.scalar.dma_start(out=b_rows[0:ROW_TILES, :], in_=b.rearrange("(m p) -> m p", p=P))
        b_turned = psum.tile([P, P], F32, name="b_turned")
        nc.tensor.transpose(b_turned[:], b_rows[:], identity[:])

        w_raw = keep.tile([P, PASSES, PACK, M], F32, name="w_raw")
        nc.sync.dma_start(
            out=w_raw[:].rearrange("p a i n -> p a (i n)"),
            in_=w.rearrange("(a p i) n -> p a (i n)", a=PASSES, i=PACK),
        )
        raws = {}
        factors = []
        for h in range(HALVES):
            for load in LOADS[h]:
                a, c0, width = load
                if load == LOADS[h][-1]:
                    tag = f"last_{h}"
                elif load == LOADS[0][-2]:
                    tag = "last_but_one"
                else:
                    tag = f"raw_{a}_{c0}"
                raw = keep.tile([P, PACK, width], F32, name=f"raw_{a}_{c0}", tag=tag)
                nc.sync.dma_start(
                    out=raw[:],
                    in_=x[a * K_PASS : (a + 1) * K_PASS, c0 : c0 + width].rearrange("(p i) c -> p i c", i=PACK),
                )
                raws[load] = raw
            if h == 0:
                nc.sync.dma_start(out=offsets[:], in_=offs)
            factor = keep.tile([P, HALF], F32, name=f"factor_{h}")
            if h == 0:
                nc.sync.dma_start(out=factor[:], in_=wgo[:, 0:HALF])
            else:
                nc.sync.dma_start(out=factor[:], in_=wgo[:, HALF:S])
            factors.append(factor)

        placed = [keep.tile([P, T], F32, name=f"placed_{m}") for m in range(ROW_TILES)]
        nc.vector.memset(placed[0][:], 0.0)
        nc.gpsimd.memset(placed[1][:], 0.0)

        w_grouped = keep.tile([P, PASSES, M, PACK], BF16, name="w_grouped", align_bytes=64)
        for a in range(PASSES):
            interleave(nc.scalar.copy, w_grouped[:, a, :, :], w_raw[:, a, :, :], 0, M)
        w_codes = keep.tile([P, PASSES * M], U32, name="w_codes", align_bytes=64)
        w_scales = keep.tile([P, PASSES * M], U8, name="w_scales", align_bytes=64)
        nc.vector.quantize_mx(
            out=w_codes[:].bitcast(FP8X4),
            scales=w_scales[:],
            in_=w_grouped[:].rearrange("p a n i -> p (a n i)"),
        )

        x_codes = [keep.tile([P, S], U32, name=f"x_codes_{a}", align_bytes=64) for a in range(PASSES)]
        x_scales = [keep.tile([P, S], U8, name=f"x_scales_{a}", align_bytes=64) for a in range(PASSES)]
        grouped = {}
        for h in range(HALVES):
            for load in LOADS[h]:
                a, c0, width = load
                grouped[load] = keep.tile([P, width, PACK], BF16, name=f"grouped_{a}_{c0}", align_bytes=64)

        def copy_in(load, c0, c1, vector_columns):
            split = c0 + vector_columns
            if vector_columns > 0:
                interleave(nc.vector.tensor_copy, grouped[load], raws[load], c0, split)
            interleave(nc.scalar.copy, grouped[load], raws[load], split, c1)

        def quantize(load, c0, c1):
            a, first, width = load
            nc.vector.quantize_mx(
                out=x_codes[a][:, first + c0 : first + c1].bitcast(FP8X4),
                scales=x_scales[a][:, first + c0 : first + c1],
                in_=grouped[load][:, c0:c1, :].rearrange("p c i -> p (c i)"),
            )

        bias = keep.tile([P, ROW_TILES], F32, name="bias", tag="last_but_one")

        def multiply(m, sums, results, h, c0, width):
            for a in range(PASSES):
                w_cols = slice(a * M + m * P, a * M + (m + 1) * P)
                x_cols = slice(h * HALF + c0, h * HALF + c0 + width)
                nc.tensor.matmul_mx(
                    out=sums,
                    lhsT=w_codes[:, w_cols].bitcast(FP8X4),
                    lhsT_scale=w_scales[:, w_cols],
                    rhs=x_codes[a][:, x_cols].bitcast(FP8X4),
                    rhs_scale=x_scales[a][:, x_cols],
                    start=(a == 0),
                    stop=(a == PASSES - 1),
                )
            nc.scalar.activation(out=results[:, c0 : c0 + width], in_=sums, func=GELU, bias=bias[:, m : m + 1])

        def place(m, results, h):
            nc.vector.tensor_tensor(
                placed[m][:].indirect(offsets[:, h * LIST_COLUMNS : (h + 1) * LIST_COLUMNS]),
                results[:],
                factors[h][:],
                MULT,
            )

        def first_row_tile(h):
            results = keep.tile([P, HALF], F32, name=f"results_0_{h}", tag=f"last_{h}")
            for block in BLOCKS[h]:
                c0, width = block
                if block == BLOCKS[h][-1]:
                    sums = psum.tile([P, HALF], F32, name=f"sums_0_{h}_last", tag="late")
                else:
                    sums = psum.tile([P, BANK], F32, name=f"sums_0_{h}_{c0}", tag=f"sums_{c0}")
                multiply(0, sums[:, 0:width], results, h, c0, width)
            return results

        def second_row_tile(h):
            results = keep.tile([P, HALF], F32, name=f"results_1_{h}")
            sums = psum.tile([P, HALF], F32, name=f"sums_1_{h}", tag="late")
            for c0 in range(0, HALF, BANK):
                multiply(1, sums[:, c0 : c0 + BANK], results, h, c0, BANK)
            return results

        whole, wide, narrow, last = LOADS[0]
        copy_in(whole, 0, 512, 320)
        quantize(whole, 0, 512)
        copy_in(whole, 512, 1024, 320)
        quantize(whole, 512, 1024)
        copy_in(wide, 0, 512, 320)
        quantize(wide, 0, 512)
        copy_in(narrow, 0, 384, 224)
        quantize(narrow, 0, 256)
        quantize(narrow, 256, 384)
        nc.scalar.copy(out=bias[:], in_=b_turned[:, 0:ROW_TILES])
        copy_in(last, 0, 128, 64)
        quantize(last, 0, 128)
        place(0, first_row_tile(0), 0)
        results = second_row_tile(0)

        for load in LOADS[1]:
            copy_in(load, 0, 512, 0)
        quantize(LOADS[1][0], 0, 512)
        place(1, results, 0)
        quantize(LOADS[1][1], 0, 512)
        quantize(LOADS[1][2], 0, 512)
        quantize(LOADS[1][3], 0, 256)
        quantize(LOADS[1][3], 256, 384)
        quantize(LOADS[1][3], 384, 512)
        place(0, first_row_tile(1), 1)
        nc.sync.dma_start(out=out[0:P, :], in_=placed[0][:])
        place(1, second_row_tile(1), 1)
        nc.sync.dma_start(out=out[P:M, :], in_=placed[1][:])
